import numpy as np
import ml_dtypes


def mxq(x, axis, fmt="e4m3"):
    dtype, down = {"e4m3": (ml_dtypes.float8_e4m3fn, 7), "e5m2": (ml_dtypes.float8_e5m2, 14)}[fmt]
    v = np.moveaxis(np.asarray(x, np.float32).astype(ml_dtypes.bfloat16).astype(np.float64), axis, -1)
    blocks = v.reshape(v.shape[:-1] + (-1, 32))
    amax = np.abs(blocks).max(-1, keepdims=True)
    byte = np.maximum(np.where(amax > 0, np.frexp(amax)[1] - 1 + 127, 0) - down, 1)
    scale = np.exp2(byte - 127.0)
    codes = (blocks / scale).astype(np.float32).astype(dtype).astype(np.float64)
    return np.moveaxis((codes * scale).reshape(v.shape), -1, axis)


WIDE = False


def mx_kscale(k):
    if not WIDE:
        return np.ones(k)
    levels = np.array([10, -10, 5, -5, 0])
    if k % 512:
        return np.exp2(np.random.permutation(np.resize(levels, k // 32))).repeat(32)
    a = np.empty((k // 512, 16))
    for p in range(k // 512):
        a[p, :8] = np.random.permutation(np.resize(levels, 8))
        for g in range(8):
            far = levels[np.abs(levels - a[p, g]) >= 10]
            a[p, g + 8] = far[np.random.randint(len(far))]
    return np.exp2(a.ravel()).repeat(32)


def f64(x):
    return np.asarray(x).astype(np.float64)


def striped(idx):
    return np.tile(idx.reshape(-1, 16).T, (8, 1)).astype(np.uint16)


def unstriped(offs):
    return offs[:16].T.reshape(-1).astype(np.int64)


def striped8(idx):
    return np.concatenate([x.reshape(-1, 16).T for x in idx]).astype(np.uint16)


def runs(offs, k):
    lists = np.stack([offs[16 * r : 16 * r + 16].T.reshape(-1) for r in range(8)]).astype(np.int64)
    return lists[np.arange(k) % 512 // 64]


def pack_weight(w):
    k, n = w.shape
    w = f64(np.asarray(w, np.float32).astype(ml_dtypes.bfloat16)).reshape(k // 32, 32, n)
    amax = np.abs(w).max(1)
    byte = np.clip(np.where(amax > 0, np.frexp(amax)[1] - 1 + 127 - 7, 1), 1, 254)
    scaled = (w * np.exp2(127.0 - byte)[:, None, :]).reshape(k, n).astype(np.float32)
    words = np.ascontiguousarray(scaled.reshape(k // 512, 128, 4, n).transpose(0, 1, 3, 2)).astype(ml_dtypes.float8_e4m3fn).view(np.uint8)
    return words, np.ascontiguousarray(byte.astype(np.uint8).reshape(k // 512, 16, n))


def unpack_weight(words, scales):
    g, p, n, _ = words.shape
    vals = np.ascontiguousarray(words).view(ml_dtypes.float8_e4m3fn).astype(np.float64) * np.repeat(np.exp2(scales.astype(np.float64) - 127.0), 8, axis=1)[..., None]
    return vals.transpose(0, 1, 3, 2).reshape(g * 512, n)


K, T, S, N, G, H, J = 512, 1024, 256, 512, 2048, 512, 512


def setup_inputs():
    n = np.random.standard_normal
    s = mx_kscale(K)[:, None]
    u = mx_kscale(K)
    packed_xT = pack_weight(n((K, T)) * s)
    packed_dT = pack_weight(n((K, G)) / s)
    return {
        "x_words": packed_xT[0],
        "x_scales": packed_xT[1],
        "d_words": packed_dT[0],
        "d_scales": packed_dT[1],
        "tab": n((H, J)).astype(np.float32),
        "gn": (np.random.uniform(0.5, 1.5, (H, 1)) * u[:, None]).astype(np.float32),
        "gm": (np.random.uniform(0.5, 1.5, (H, 1)) * u[:, None]).astype(np.float32),
        "w1": (n((H, N)) / np.sqrt(2 * H) / u[:, None]).astype(np.float32),
        "w2": (n((H, N)) / np.sqrt(2 * H) / u[:, None]).astype(np.float32),
        "offs": striped(np.random.permutation(T)[:S]),
        "k1": striped8(np.random.randint(0, G, (8, H))),
        "two": striped(np.random.permutation(T)[:S]),
        "k2": striped8(np.random.randint(0, G, (8, H))),
        "n1": striped(np.random.permutation(S)),
        "n2": striped(np.random.permutation(S)),
        "n3": striped(np.random.randint(0, J, S)),
        "n4": striped(np.random.permutation(S)),
        "n5": striped(np.random.permutation(S)),
        "n6": striped(np.random.permutation(S)),
        "n7": striped(np.random.permutation(S)),
    }


def reference(x_words, x_scales, d_words, d_scales, tab, gn, gm, w1, w2, offs, k1, two, k2, n1, n2, n3, n4, n5, n6, n7):
    d_k1 = unpack_weight(d_words, d_scales)[np.arange(K)[:, None], runs(k1, K)]
    xq = unpack_weight(x_words, x_scales)[:, unstriped(offs)]
    a = 0.0625 * (d_k1.T @ xq)
    z = f64(gn) * ((a - a[:, unstriped(n1)]) / (np.abs(a[:, unstriped(n2)] - a) + 0.5))
    d_k2 = unpack_weight(d_words, d_scales)[np.arange(K)[:, None], runs(k2, K)]
    x_two = unpack_weight(x_words, x_scales)[:, unstriped(two)]
    b = 0.0625 * (d_k2.T @ x_two)
    z2 = f64(gm) * (np.abs(b - b[:, unstriped(n4)] - f64(tab)[:, unstriped(n3)]))
    h = mxq(f64(w1), 0, "e4m3").T @ mxq(z, 0, "e4m3") + mxq(f64(w2), 0, "e4m3").T @ mxq(z2, 0, "e4m3")
    return 0.75 * (h * h[:, unstriped(n5)] + h[:, unstriped(n6)] * h[:, unstriped(n7)])

@@ -1,0 +1,264 @@
+from contextlib import ExitStack
+
+import concourse.mybir as mybir
+
+K, T, S, N, G, H, J = 512, 1024, 256, 512, 2048, 512, 512
+FLOPS = 4 * 2 * 512 * 512 * 256
+
+F32 = mybir.dt.float32
+BF16 = mybir.dt.bfloat16
+U32 = mybir.dt.uint32
+I32 = mybir.dt.int32
+U16 = mybir.dt.uint16
+U8 = mybir.dt.uint8
+FP8X4 = mybir.dt.float8_e4m3fn_x4
+ALU = mybir.AluOpType
+ACT = mybir.ActivationFunctionType
+
+P = 128
+PACK = 4
+SPARE = 8
+
+
+def tile_picked_pqjfrackindddot_none_p_kernel(
+    tc, x_words, x_scales, d_words, d_scales, tab, gn, gm, w1, w2,
+    offs, k1, two, k2, n1, n2, n3, n4, n5, n6, n7, out,
+):
+    nc = tc.nc
+    with ExitStack() as ctx:
+        keep = ctx.enter_context(tc.tile_pool(name="keep", bufs=1))
+        reuse = ctx.enter_context(tc.tile_pool(name="reuse", bufs=1))
+        psum = ctx.enter_context(tc.psum_pool(name="psum", bufs=1))
+
+        def sb(name, width, dtype, tag=None):
+            return keep.tile([P, width], dtype, name=name, tag=tag or name, align_bytes=64)
+
+        def placed(name, width, dtype, offset):
+            return reuse.tile([P, width], dtype, name=name, offset=offset, align_bytes=64)
+
+        def load_list(name, src):
+            tile = keep.tile([P, src.shape[1]], U16, name=name)
+            nc.sync.dma_start(tile[:], src)
+            return tile
+
+        def load_scales(name, src, width):
+            tile = sb(name, width, U8)
+            rows = src[0].bitcast(I32).unsqueeze(1).to_broadcast([16, 8, width // 4])
+            nc.sync.dma_start(tile[:].bitcast(I32), rows)
+            return tile
+
+        def load_words(name, src, width):
+            tile = sb(name, width, I32)
+            nc.sync.dma_start(tile[:], src[0].rearrange("p n t -> p (n t)").bitcast(I32))
+            return tile
+
+        def load_weight(name, src, tag=None):
+            tile = sb(name, PACK * N, F32, tag)
+            nc.sync.dma_start(tile[:], src.rearrange("(p t) n -> p (t n)", t=PACK))
+            return tile
+
+        def load_gain(name, src, offset):
+            tile = placed(name, PACK, F32, offset)
+            nc.sync.dma_start(tile[:], src.rearrange("(p t) o -> p (t o)", t=PACK))
+            return tile
+
+        d_sc = load_scales("d_sc", d_scales, G)
+        k2_l = load_list("k2_l", k2)
+        k1_l = load_list("k1_l", k1)
+        x_sc = load_scales("x_sc", x_scales, T)
+        two_l = load_list("two_l", two)
+        offs_l = load_list("offs_l", offs)
+        row = 4 * J
+        x_w = placed("x_w", T, I32, 2 * row + 128)
+        nc.sync.dma_start(x_w[:], x_words[0].rearrange("p n t -> p (n t)").bitcast(I32))
+        d_w = load_words("d_w", d_words, G)
+        n4_l = load_list("n4_l", n4)
+        n3_l = load_list("n3_l", n3)
+        n2_l = load_list("n2_l", n2)
+        w1_raw = load_weight("w1_raw", w1)
+        n1_l = load_list("n1_l", n1)
+        n7_l = load_list("n7_l", n7)
+        n5_l = load_list("n5_l", n5)
+        n6_l = load_list("n6_l", n6)
+
+        def windows(name):
+            tiles = [sb(name + str(t), S + SPARE, F32) for t in range(PACK)]
+            for tile in tiles:
+                nc.gpsimd.memset(tile[:, S:], 0.0)
+            return tiles
+
+        a_win = windows("a_win")
+        b_win = windows("b_win")
+        h_win = windows("h_win")
+        eight = sb("eight", 1, F32)
+        nc.gpsimd.memset(eight[:], 8.0)
+
+        sc_picked = placed("sc_picked", 2 * H + 2 * S, U8, row // 2)
+        nc.vector.tensor_copy(sc_picked[:, H : 2 * H], d_sc[:].indirect(k2_l[:]))
+        nc.vector.tensor_copy(sc_picked[:, 0:H], d_sc[:].indirect(k1_l[:]))
+        nc.vector.tensor_copy(sc_picked[:, 2 * H + S :], x_sc[:].indirect(two_l[:]))
+        nc.vector.tensor_copy(sc_picked[:, 2 * H : 2 * H + S], x_sc[:].indirect(offs_l[:]))
+        sc = sb("sc", 2 * H + 2 * S, U8)
+        nc.vector.tensor_copy(
+            sc[:, : 2 * H].rearrange("p (l t m) -> p l t m", l=2, t=PACK),
+            sc_picked[:, : 2 * H].rearrange("p (l m t) -> p l t m", l=2, t=PACK),
+        )
+        nc.vector.tensor_copy(sc[:, 2 * H :].bitcast(I32), sc_picked[:, 2 * H :].bitcast(I32))
+        for i in range(1, 4):
+            nc.sync.dma_start(sc[i:P:32, :].bitcast(I32), sc[8 * i : P : 32, :].bitcast(I32))
+
+        tab_rows = tab.rearrange("(p t) c -> p t c", t=PACK)
+
+        def load_tab(t):
+            tile = placed("tab_win" + str(t), J, F32, t * row + (128 if t else 0))
+            nc.sync.dma_start(tile[:], tab_rows[:, t, :])
+            return tile
+
+        tab_win = [load_tab(0), load_tab(1)]
+        gm_t = load_gain("gm_t", gm, row)
+        gn_t = load_gain("gn_t", gn, row + 64)
+
+        def interleaved(tile):
+            return tile[:].rearrange("p (c i t) -> p c t i", i=4, t=PACK)
+
+        def planes(tile):
+            return tile[:].rearrange("p (t c i) -> p c t i", i=4, t=PACK)
+
+        def quantize(name, grouped, width):
+            codes = sb(name + "_codes", width, U32)
+            scales = sb(name + "_scales", width, U8)
+            nc.vector.quantize_mx(out=codes[:].bitcast(FP8X4), scales=scales[:], in_=grouped[:])
+            return codes, scales
+
+        w1_bf = sb("w1_bf", PACK * N, BF16)
+        nc.scalar.copy(interleaved(w1_bf), planes(w1_raw))
+
+        def pick_tokens(name, x_list):
+            tokens = sb(name + "_tokens", S, U32)
+            nc.vector.tensor_copy(tokens[:], x_w[:].bitcast(U32).indirect(x_list[:]))
+            return tokens
+
+        def first_product(name, d_list, tokens, side, picked):
+            nc.vector.tensor_copy(picked[:], d_w[:].bitcast(U32).indirect(d_list[:]))
+            dealt = sb(name + "_dealt", H, I32)
+            nc.vector.tensor_copy(planes(dealt), picked[:].bitcast(I32).rearrange("p (c i t) -> p c t i", i=4, t=PACK))
+            banks = [psum.tile([P, 2 * S], F32, name=name + "_bank" + str(u)) for u in range(2)]
+            for t in range(PACK):
+                nc.tensor.matmul_mx(
+                    out=banks[t // 2][:, (t % 2) * S : (t % 2 + 1) * S],
+                    lhsT=dealt[:, t * P : (t + 1) * P].bitcast(FP8X4),
+                    lhsT_scale=sc[:, side * H + t * P : side * H + (t + 1) * P],
+                    rhs=tokens[:].bitcast(FP8X4),
+                    rhs_scale=sc[:, 2 * H + side * S : 2 * H + (side + 1) * S],
+                    start=True,
+                    stop=True,
+                )
+            return banks
+
+        b_tokens = pick_tokens("b", two_l)
+        a_tokens = pick_tokens("a", offs_l)
+        tab_win.extend([load_tab(2), load_tab(3)])
+        b_bank = first_product("b", k2_l, b_tokens, 1, sb("b_picked", H, U32, "staging"))
+        a_bank = first_product("a", k1_l, a_tokens, 0, sb("a_picked", H, U32, "staging"))
+        w2_raw = load_weight("w2_raw", w2, "d_w")
+        w1_codes, w1_scales = quantize("w1", w1_bf, N)
+
+        def col(t):
+            return slice(t * S, (t + 1) * S)
+
+        def half(u):
+            return slice(2 * u * S, 2 * (u + 1) * S)
+
+        def in_bank(banks, t):
+            return banks[t // 2][:, (t % 2) * S : (t % 2 + 1) * S]
+
+        bt_n4 = sb("bt_n4", PACK * S, F32)
+        taken = sb("taken", PACK * S, F32)
+        left = sb("left", PACK * S, F32)
+        left_size = sb("left_size", PACK * S, F32)
+        at_n1 = sb("at_n1", PACK * S, F32)
+        at_n2 = sb("at_n2", PACK * S, F32)
+        diff = sb("diff", PACK * S, F32)
+        numer = sb("numer", PACK * S, F32)
+        size = sb("size", PACK * S, F32)
+        root = sb("root", PACK * S, F32)
+        part = sb("part", PACK * S, F32)
+        for u in range(2):
+            for t in (2 * u, 2 * u + 1):
+                nc.scalar.activation(b_win[t][:, :S], in_bank(b_bank, t), ACT.Copy, scale=0.0625)
+            for t in (2 * u, 2 * u + 1):
+                nc.scalar.activation(bt_n4[:, col(t)], b_win[t][:].indirect(n4_l[:]), ACT.Copy)
+                nc.vector.tensor_tensor(taken[:, col(t)], tab_win[t][:].indirect(n3_l[:]), b_win[t][:, :S], ALU.subtract)
+            nc.vector.tensor_tensor(left[:, half(u)], taken[:, half(u)], bt_n4[:, half(u)], ALU.add)
+
+        for u in range(2):
+            for t in (2 * u, 2 * u + 1):
+                nc.scalar.copy(a_win[t][:, :S], in_bank(a_bank, t))
+            for t in (2 * u, 2 * u + 1):
+                nc.scalar.activation(at_n2[:, col(t)], a_win[t][:].indirect(n2_l[:]), ACT.Copy)
+            nc.vector.tensor_tensor(diff[:, half(u)], at_n2[:, half(u)], a_bank[u][:], ALU.subtract)
+
+        nc.scalar.activation(left_size[:], left[:], ACT.Abs)
+        z2_bf = sb("z2_bf", PACK * S, BF16)
+        gm_wide = gm_t[:].unsqueeze(1).unsqueeze(3).to_broadcast([P, S // 4, PACK, 4])
+        nc.vector.tensor_tensor(interleaved(z2_bf), planes(left_size), gm_wide, ALU.mult)
+        for u in range(2):
+            nc.vector.scalar_tensor_tensor(size[:, half(u)], diff[:, half(u)], -1.0, diff[:, half(u)], ALU.mult, ALU.max)
+        z2_codes, z2_scales = quantize("z2", z2_bf, S)
+
+        for u in range(2):
+            for t in (2 * u, 2 * u + 1):
+                nc.scalar.activation(at_n1[:, col(t)], a_win[t][:].indirect(n1_l[:]), ACT.Copy)
+            nc.scalar.activation(root[:, half(u)], size[:, half(u)], ACT.Abs_reciprocal_sqrt, bias=eight[:])
+            nc.vector.tensor_tensor(numer[:, half(u)], a_bank[u][:], at_n1[:, half(u)], ALU.subtract)
+            for t in (2 * u, 2 * u + 1):
+                nc.vector.scalar_tensor_tensor(
+                    part[:, col(t)], numer[:, col(t)], gn_t[:, t : t + 1], root[:, col(t)], ALU.mult, ALU.mult
+                )
+
+        w2_bf = sb("w2_bf", PACK * N, BF16, "size")
+        w2_codes = sb("w2_codes", N, U32)
+        w2_scales = sb("w2_scales", N, U8)
+        wide = N // 8
+        for u in range(2):
+            nc.scalar.copy(interleaved(w2_bf)[:, u * wide : (u + 1) * wide], planes(w2_raw)[:, u * wide : (u + 1) * wide])
+
+        def quantize_w2(u):
+            nc.vector.quantize_mx(
+                out=w2_codes[:, u * N // 2 : (u + 1) * N // 2].bitcast(FP8X4),
+                scales=w2_scales[:, u * N // 2 : (u + 1) * N // 2],
+                in_=w2_bf[:, u * 2 * N : (u + 1) * 2 * N],
+            )
+
+        z_bf = sb("z_bf", PACK * S, BF16)
+        nc.vector.tensor_tensor(interleaved(z_bf), planes(part), planes(root), ALU.mult)
+        quantize_w2(0)
+        z_codes, z_scales = quantize("z", z_bf, S)
+        quantize_w2(1)
+
+        h_bank = [psum.tile([P, S], F32, name="h_bank" + str(m)) for m in range(PACK)]
+        for m in range(PACK):
+            for first, (wc, ws, zc, zs) in ((True, (w2_codes, w2_scales, z2_codes, z2_scales)), (False, (w1_codes, w1_scales, z_codes, z_scales))):
+                nc.tensor.matmul_mx(
+                    out=h_bank[m][:],
+                    lhsT=wc[:, m * P : (m + 1) * P].bitcast(FP8X4),
+                    lhsT_scale=ws[:, m * P : (m + 1) * P],
+                    rhs=zc[:].bitcast(FP8X4),
+                    rhs_scale=zs[:],
+                    start=first,
+                    stop=not first,
+                )
+
+        for m in range(PACK):
+            at_n7 = sb("at_n7_" + str(m), S, F32)
+            at_n5 = sb("at_n5_" + str(m), S, F32)
+            far = sb("far" + str(m), S, F32)
+            near = sb("near" + str(m), S, F32)
+            result = sb("result" + str(m), S, F32)
+            nc.vector.tensor_copy(h_win[m][:, :S], h_bank[m][:])
+            nc.scalar.activation(at_n7[:], h_win[m][:].indirect(n7_l[:]), ACT.Copy)
+            nc.scalar.activation(at_n5[:], h_win[m][:].indirect(n5_l[:]), ACT.Copy)
+            nc.vector.tensor_tensor(far[:], h_win[m][:].indirect(n6_l[:]), at_n7[:], ALU.mult)
+            nc.vector.scalar_tensor_tensor(near[:], at_n5[:], 0.75, h_bank[m][:], ALU.mult, ALU.mult)
+            nc.vector.scalar_tensor_tensor(result[:], far[:], 0.75, near[:], ALU.mult, ALU.add)
+            nc.sync.dma_start(out[m * P : (m + 1) * P, :], result[:])

@@ -52,71 +52,78 @@ def tile_picked_pqjfrackindddot_none_p_kernel(
             nc.sync.dma_start(tile[:], src[0].rearrange("p n t -> p (n t)").bitcast(I32))
             return tile
 
-        def load_weight(name, src, tag=None):
-            tile = sb(name, PACK * N, F32, tag)
-            nc.sync.dma_start(tile[:], src.rearrange("(p t) n -> p (t n)", t=PACK))
-            return tile
+        def rows_of_tile(src, t):
+            return src.rearrange("(b t r) c -> t b r c", t=PACK, r=8)[t]
+
+        def load_weight(tile, src, tiles):
+            for t in tiles:
+                nc.sync.dma_start(tile[:, t * N : (t + 1) * N], rows_of_tile(src, t))
 
         def load_gain(name, src, offset):
-            tile = placed(name, PACK, F32, offset)
-            nc.sync.dma_start(tile[:], src.rearrange("(p t) o -> p (t o)", t=PACK))
-            return tile
+            spread = placed(name + "_spread", PACK * 8, F32, offset)
+            with nc.allow_non_contiguous_dma(reason="one gain for each partition"):
+                for t in range(PACK):
+                    nc.sync.dma_start(spread[:, 8 * t : 8 * t + 1], rows_of_tile(src, t))
+            return spread[:, 0 : PACK * 8 : 8]
 
-        d_sc = load_scales("d_sc", d_scales, G)
-        k2_l = load_list("k2_l", k2)
-        k1_l = load_list("k1_l", k1)
         x_sc = load_scales("x_sc", x_scales, T)
         two_l = load_list("two_l", two)
         offs_l = load_list("offs_l", offs)
+        d_sc = load_scales("d_sc", d_scales, G)
+        k2_l = load_list("k2_l", k2)
+        k1_l = load_list("k1_l", k1)
         row = 4 * J
         x_w = placed("x_w", T, I32, 2 * row + 128)
         nc.sync.dma_start(x_w[:], x_words[0].rearrange("p n t -> p (n t)").bitcast(I32))
         d_w = load_words("d_w", d_words, G)
+        w2_raw = sb("w2_raw", PACK * N, F32)
+        load_weight(w2_raw, w2, (0, 1))
         n4_l = load_list("n4_l", n4)
         n3_l = load_list("n3_l", n3)
         n2_l = load_list("n2_l", n2)
-        w1_raw = load_weight("w1_raw", w1)
         n1_l = load_list("n1_l", n1)
+        load_weight(w2_raw, w2, (2, 3))
         n7_l = load_list("n7_l", n7)
         n5_l = load_list("n5_l", n5)
         n6_l = load_list("n6_l", n6)
 
-        def windows(name):
-            tiles = [sb(name + str(t), S + SPARE, F32) for t in range(PACK)]
+        def windows(name, base=None):
+            if base is None:
+                tiles = [sb(name + str(t), S + SPARE, F32) for t in range(PACK)]
+            else:
+                tiles = [placed(name + str(t), S + SPARE, F32, base + t * 1088) for t in range(PACK)]
             for tile in tiles:
                 nc.gpsimd.memset(tile[:, S:], 0.0)
             return tiles
 
-        a_win = windows("a_win")
-        b_win = windows("b_win")
-        h_win = windows("h_win")
         eight = sb("eight", 1, F32)
         nc.gpsimd.memset(eight[:], 8.0)
+        warm = sb("warm", 1, F32)
+        nc.scalar.activation(warm[:], eight[:], ACT.Abs_reciprocal_sqrt, bias=eight[:])
+        a_win = windows("a_win", 6 * row)
+        b_win = windows("b_win")
+        h_win = windows("h_win")
 
         sc_picked = placed("sc_picked", 2 * H + 2 * S, U8, row // 2)
-        nc.vector.tensor_copy(sc_picked[:, H : 2 * H], d_sc[:].indirect(k2_l[:]))
-        nc.vector.tensor_copy(sc_picked[:, 0:H], d_sc[:].indirect(k1_l[:]))
         nc.vector.tensor_copy(sc_picked[:, 2 * H + S :], x_sc[:].indirect(two_l[:]))
         nc.vector.tensor_copy(sc_picked[:, 2 * H : 2 * H + S], x_sc[:].indirect(offs_l[:]))
+        nc.vector.tensor_copy(sc_picked[:, H : 2 * H], d_sc[:].indirect(k2_l[:]))
+        nc.vector.tensor_copy(sc_picked[:, 0:H], d_sc[:].indirect(k1_l[:]))
         sc = sb("sc", 2 * H + 2 * S, U8)
         nc.vector.tensor_copy(
-            sc[:, : 2 * H].rearrange("p (l t m) -> p l t m", l=2, t=PACK),
-            sc_picked[:, : 2 * H].rearrange("p (l m t) -> p l t m", l=2, t=PACK),
+            sc[:, : 2 * H].bitcast(I32).rearrange("p (l t b w) -> p l t b w", l=2, t=PACK, w=2),
+            sc_picked[:, : 2 * H].bitcast(I32).rearrange("p (l b t w) -> p l t b w", l=2, t=PACK, w=2),
         )
         nc.vector.tensor_copy(sc[:, 2 * H :].bitcast(I32), sc_picked[:, 2 * H :].bitcast(I32))
         for i in range(1, 4):
             nc.sync.dma_start(sc[i:P:32, :].bitcast(I32), sc[8 * i : P : 32, :].bitcast(I32))
 
-        tab_rows = tab.rearrange("(p t) c -> p t c", t=PACK)
-
         def load_tab(t):
             tile = placed("tab_win" + str(t), J, F32, t * row + (128 if t else 0))
-            nc.sync.dma_start(tile[:], tab_rows[:, t, :])
+            nc.sync.dma_start(tile[:], rows_of_tile(tab, t))
             return tile
 
         tab_win = [load_tab(0), load_tab(1)]
-        gm_t = load_gain("gm_t", gm, row)
-        gn_t = load_gain("gn_t", gn, row + 64)
 
         def interleaved(tile):
             return tile[:].rearrange("p (c i t) -> p c t i", i=4, t=PACK)
@@ -124,28 +131,33 @@ def tile_picked_pqjfrackindddot_none_p_kernel(
         def planes(tile):
             return tile[:].rearrange("p (t c i) -> p c t i", i=4, t=PACK)
 
-        def quantize(name, grouped, width):
-            codes = sb(name + "_codes", width, U32)
+        def quantize(name, grouped, width, offset=None):
+            if offset is None:
+                codes = sb(name + "_codes", width, U32)
+            else:
+                codes = placed(name + "_codes", width, U32, offset)
             scales = sb(name + "_scales", width, U8)
             nc.vector.quantize_mx(out=codes[:].bitcast(FP8X4), scales=scales[:], in_=grouped[:])
             return codes, scales
 
-        w1_bf = sb("w1_bf", PACK * N, BF16)
-        nc.scalar.copy(interleaved(w1_bf), planes(w1_raw))
+        w2_bf = sb("w2_bf", PACK * N, BF16)
+        nc.scalar.copy(interleaved(w2_bf), planes(w2_raw))
 
         def pick_tokens(name, x_list):
             tokens = sb(name + "_tokens", S, U32)
             nc.vector.tensor_copy(tokens[:], x_w[:].bitcast(U32).indirect(x_list[:]))
             return tokens
 
-        def first_product(name, d_list, tokens, side, picked):
+        def first_product(name, d_list, tokens, side, picked, outs):
             nc.vector.tensor_copy(picked[:], d_w[:].bitcast(U32).indirect(d_list[:]))
             dealt = sb(name + "_dealt", H, I32)
-            nc.vector.tensor_copy(planes(dealt), picked[:].bitcast(I32).rearrange("p (c i t) -> p c t i", i=4, t=PACK))
-            banks = [psum.tile([P, 2 * S], F32, name=name + "_bank" + str(u)) for u in range(2)]
+            nc.vector.tensor_copy(
+                dealt[:].rearrange("p (t b r) -> p t b r", t=PACK, r=8),
+                picked[:].bitcast(I32).rearrange("p (b t r) -> p t b r", t=PACK, r=8),
+            )
             for t in range(PACK):
                 nc.tensor.matmul_mx(
-                    out=banks[t // 2][:, (t % 2) * S : (t % 2 + 1) * S],
+                    out=outs[t],
                     lhsT=dealt[:, t * P : (t + 1) * P].bitcast(FP8X4),
                     lhsT_scale=sc[:, side * H + t * P : side * H + (t + 1) * P],
                     rhs=tokens[:].bitcast(FP8X4),
@@ -153,15 +165,20 @@ def tile_picked_pqjfrackindddot_none_p_kernel(
                     start=True,
                     stop=True,
                 )
-            return banks
 
         b_tokens = pick_tokens("b", two_l)
         a_tokens = pick_tokens("a", offs_l)
         tab_win.extend([load_tab(2), load_tab(3)])
-        b_bank = first_product("b", k2_l, b_tokens, 1, sb("b_picked", H, U32, "staging"))
-        a_bank = first_product("a", k1_l, a_tokens, 0, sb("a_picked", H, U32, "staging"))
-        w2_raw = load_weight("w2_raw", w2, "d_w")
-        w1_codes, w1_scales = quantize("w1", w1_bf, N)
+        b_bank = [psum.tile([P, S], F32, name="b_bank" + str(t), tag="single" + str(t)) for t in range(PACK)]
+        a_bank = [psum.tile([P, 2 * S], F32, name="a_bank" + str(u)) for u in range(2)]
+        a_sums = [a_bank[t // 2][:, (t % 2) * S : (t % 2 + 1) * S] for t in range(PACK)]
+        first_product("b", k2_l, b_tokens, 1, placed("b_picked", H, U32, 12 * row), [bank[:] for bank in b_bank])
+        gm_t = sb("gm_t", PACK, F32)
+        nc.gpsimd.tensor_copy(gm_t[:], load_gain("gm_t", gm, 12 * row))
+        gn_t = load_gain("gn_t", gn, 12 * row + 128)
+        first_product("a", k1_l, a_tokens, 0, placed("a_picked", H, U32, 12 * row + row // 2), a_sums)
+        w1_raw = sb("w1_raw", PACK * N, F32, "d_w")
+        load_weight(w1_raw, w1, range(PACK))
 
         def col(t):
             return slice(t * S, (t + 1) * S)
@@ -169,93 +186,103 @@ def tile_picked_pqjfrackindddot_none_p_kernel(
         def half(u):
             return slice(2 * u * S, 2 * (u + 1) * S)
 
-        def in_bank(banks, t):
-            return banks[t // 2][:, (t % 2) * S : (t % 2 + 1) * S]
-
         bt_n4 = sb("bt_n4", PACK * S, F32)
         taken = sb("taken", PACK * S, F32)
         left = sb("left", PACK * S, F32)
         left_size = sb("left_size", PACK * S, F32)
         at_n1 = sb("at_n1", PACK * S, F32)
         at_n2 = sb("at_n2", PACK * S, F32)
-        diff = sb("diff", PACK * S, F32)
         numer = sb("numer", PACK * S, F32)
-        size = sb("size", PACK * S, F32)
-        root = sb("root", PACK * S, F32)
         part = sb("part", PACK * S, F32)
+        for t in range(PACK):
+            nc.scalar.activation(b_win[t][:, :S], b_bank[t][:], ACT.Copy, scale=0.0625)
         for u in range(2):
-            for t in (2 * u, 2 * u + 1):
-                nc.scalar.activation(b_win[t][:, :S], in_bank(b_bank, t), ACT.Copy, scale=0.0625)
             for t in (2 * u, 2 * u + 1):
                 nc.scalar.activation(bt_n4[:, col(t)], b_win[t][:].indirect(n4_l[:]), ACT.Copy)
                 nc.vector.tensor_tensor(taken[:, col(t)], tab_win[t][:].indirect(n3_l[:]), b_win[t][:, :S], ALU.subtract)
-            nc.vector.tensor_tensor(left[:, half(u)], taken[:, half(u)], bt_n4[:, half(u)], ALU.add)
-
+        w2_codes, w2_scales = quantize("w2", w2_bf, N, 13 * row)
         for u in range(2):
-            for t in (2 * u, 2 * u + 1):
-                nc.scalar.copy(a_win[t][:, :S], in_bank(a_bank, t))
-            for t in (2 * u, 2 * u + 1):
-                nc.scalar.activation(at_n2[:, col(t)], a_win[t][:].indirect(n2_l[:]), ACT.Copy)
-            nc.vector.tensor_tensor(diff[:, half(u)], at_n2[:, half(u)], a_bank[u][:], ALU.subtract)
+            nc.vector.tensor_tensor(left[:, half(u)], taken[:, half(u)], bt_n4[:, half(u)], ALU.add)
+        for u in range(2):
+            nc.vector.scalar_tensor_tensor(
+                left_size[:, half(u)], left[:, half(u)], -1.0, left[:, half(u)], ALU.mult, ALU.max
+            )
 
-        nc.scalar.activation(left_size[:], left[:], ACT.Abs)
+        size = [sb("size0", 2 * S, F32), placed("size1", 2 * S, F32, 9 * row + row // 2)]
+        for t in range(PACK):
+            nc.scalar.copy(a_win[t][:, :S], a_sums[t])
+        for t in range(PACK):
+            nc.scalar.activation(at_n2[:, col(t)], a_win[t][:].indirect(n2_l[:]), ACT.Copy)
+
+        def distance(u, tag):
+            diff = sb("diff" + str(u), 2 * S, F32, tag)
+            nc.vector.tensor_tensor(diff[:], at_n2[:, half(u)], a_bank[u][:], ALU.subtract)
+            nc.vector.scalar_tensor_tensor(size[u][:], diff[:], -1.0, diff[:], ALU.mult, ALU.max)
+
+        distance(0, "taken")
         z2_bf = sb("z2_bf", PACK * S, BF16)
         gm_wide = gm_t[:].unsqueeze(1).unsqueeze(3).to_broadcast([P, S // 4, PACK, 4])
         nc.vector.tensor_tensor(interleaved(z2_bf), planes(left_size), gm_wide, ALU.mult)
-        for u in range(2):
-            nc.vector.scalar_tensor_tensor(size[:, half(u)], diff[:, half(u)], -1.0, diff[:, half(u)], ALU.mult, ALU.max)
         z2_codes, z2_scales = quantize("z2", z2_bf, S)
+        distance(1, "left_size")
 
+        h_bank = [psum.tile([P, S], F32, name="h_bank" + str(m), tag="single" + str(m)) for m in range(PACK)]
+
+        def last_product(codes, scales, moving, moving_scales, first):
+            for m in range(PACK):
+                nc.tensor.matmul_mx(
+                    out=h_bank[m][:],
+                    lhsT=codes[:, m * P : (m + 1) * P].bitcast(FP8X4),
+                    lhsT_scale=scales[:, m * P : (m + 1) * P],
+                    rhs=moving[:].bitcast(FP8X4),
+                    rhs_scale=moving_scales[:],
+                    start=first,
+                    stop=not first,
+                )
+
+        last_product(w2_codes, w2_scales, z2_codes, z2_scales, True)
+
+        root = placed("root", PACK * S, F32, 6 * row + 2 * 1088 - 2 * row)
         for u in range(2):
             for t in (2 * u, 2 * u + 1):
                 nc.scalar.activation(at_n1[:, col(t)], a_win[t][:].indirect(n1_l[:]), ACT.Copy)
-            nc.scalar.activation(root[:, half(u)], size[:, half(u)], ACT.Abs_reciprocal_sqrt, bias=eight[:])
             nc.vector.tensor_tensor(numer[:, half(u)], a_bank[u][:], at_n1[:, half(u)], ALU.subtract)
+        for u in range(2):
+            nc.scalar.activation(root[:, half(u)], size[u][:], ACT.Abs_reciprocal_sqrt, bias=eight[:])
             for t in (2 * u, 2 * u + 1):
                 nc.vector.scalar_tensor_tensor(
                     part[:, col(t)], numer[:, col(t)], gn_t[:, t : t + 1], root[:, col(t)], ALU.mult, ALU.mult
                 )
 
-        w2_bf = sb("w2_bf", PACK * N, BF16, "size")
-        w2_codes = sb("w2_codes", N, U32)
-        w2_scales = sb("w2_scales", N, U8)
+        w1_codes = sb("w1_codes", N, U32, "numer")
+        w1_scales = sb("w1_scales", N, U8)
+        w1_bf = [placed("w1_bf" + str(u), 2 * N, BF16, (9 + u) * row) for u in range(2)]
         wide = N // 8
         for u in range(2):
-            nc.scalar.copy(interleaved(w2_bf)[:, u * wide : (u + 1) * wide], planes(w2_raw)[:, u * wide : (u + 1) * wide])
+            nc.scalar.copy(interleaved(w1_bf[u]), planes(w1_raw)[:, u * wide : (u + 1) * wide])
 
-        def quantize_w2(u):
+        def quantize_w1(u):
             nc.vector.quantize_mx(
-                out=w2_codes[:, u * N // 2 : (u + 1) * N // 2].bitcast(FP8X4),
-                scales=w2_scales[:, u * N // 2 : (u + 1) * N // 2],
-                in_=w2_bf[:, u * 2 * N : (u + 1) * 2 * N],
+                out=w1_codes[:, u * N // 2 : (u + 1) * N // 2].bitcast(FP8X4),
+                scales=w1_scales[:, u * N // 2 : (u + 1) * N // 2],
+                in_=w1_bf[u][:],
             )
 
         z_bf = sb("z_bf", PACK * S, BF16)
         nc.vector.tensor_tensor(interleaved(z_bf), planes(part), planes(root), ALU.mult)
-        quantize_w2(0)
+        quantize_w1(0)
         z_codes, z_scales = quantize("z", z_bf, S)
-        quantize_w2(1)
+        quantize_w1(1)
+        last_product(w1_codes, w1_scales, z_codes, z_scales, False)
 
-        h_bank = [psum.tile([P, S], F32, name="h_bank" + str(m)) for m in range(PACK)]
         for m in range(PACK):
-            for first, (wc, ws, zc, zs) in ((True, (w2_codes, w2_scales, z2_codes, z2_scales)), (False, (w1_codes, w1_scales, z_codes, z_scales))):
-                nc.tensor.matmul_mx(
-                    out=h_bank[m][:],
-                    lhsT=wc[:, m * P : (m + 1) * P].bitcast(FP8X4),
-                    lhsT_scale=ws[:, m * P : (m + 1) * P],
-                    rhs=zc[:].bitcast(FP8X4),
-                    rhs_scale=zs[:],
-                    start=first,
-                    stop=not first,
-                )
-
+            nc.vector.tensor_copy(h_win[m][:, :S], h_bank[m][:])
         for m in range(PACK):
             at_n7 = sb("at_n7_" + str(m), S, F32)
             at_n5 = sb("at_n5_" + str(m), S, F32)
             far = sb("far" + str(m), S, F32)
             near = sb("near" + str(m), S, F32)
             result = sb("result" + str(m), S, F32)
-            nc.vector.tensor_copy(h_win[m][:, :S], h_bank[m][:])
             nc.scalar.activation(at_n7[:], h_win[m][:].indirect(n7_l[:]), ACT.Copy)
             nc.scalar.activation(at_n5[:], h_win[m][:].indirect(n5_l[:]), ACT.Copy)
             nc.vector.tensor_tensor(far[:], h_win[m][:].indirect(n6_l[:]), at_n7[:], ALU.mult)

@@ -2,7 +2,7 @@ from contextlib import ExitStack
 
 import concourse.mybir as mybir
 
-K, T, S, N, G, H, J = 512, 1024, 256, 512, 2048, 512, 512
+T, S, N, G, H, J = 1024, 256, 512, 2048, 512, 512
 FLOPS = 4 * 2 * 512 * 512 * 256
 
 F32 = mybir.dt.float32
@@ -16,8 +16,21 @@ ALU = mybir.AluOpType
 ACT = mybir.ActivationFunctionType
 
 P = 128
-PACK = 4
+PLANES = 4
+BLOCK_ROWS = 8
+BLOCKS = P // BLOCK_ROWS
+QUADRANT = 32
+LIST_ROWS = 16
+RUN = 4
 SPARE = 8
+GAIN_STEP = 8
+ALIGN = 64
+
+KIB = 1024
+WINDOW_PITCH = 1088
+A_WINDOWS = 4 * KIB
+SIZE_AREA = 12 * KIB
+PICKED_AREA = 18 * KIB
 
 
 def tile_picked_pqjfrackindddot_none_p_kernel(
@@ -27,14 +40,14 @@ def tile_picked_pqjfrackindddot_none_p_kernel(
     nc = tc.nc
     with ExitStack() as ctx:
         keep = ctx.enter_context(tc.tile_pool(name="keep", bufs=1))
-        reuse = ctx.enter_context(tc.tile_pool(name="reuse", bufs=1))
+        by_hand = ctx.enter_context(tc.tile_pool(name="by_hand", bufs=1))
         psum = ctx.enter_context(tc.psum_pool(name="psum", bufs=1))
 
-        def sb(name, width, dtype, tag=None):
-            return keep.tile([P, width], dtype, name=name, tag=tag or name, align_bytes=64)
+        def sb(name, width, dtype, on=None):
+            return keep.tile([P, width], dtype, name=name, tag=on or name, align_bytes=ALIGN)
 
         def placed(name, width, dtype, offset):
-            return reuse.tile([P, width], dtype, name=name, offset=offset, align_bytes=64)
+            return by_hand.tile([P, width], dtype, name=name, offset=offset, align_bytes=ALIGN)
 
         def load_list(name, src):
             tile = keep.tile([P, src.shape[1]], U16, name=name)
@@ -43,7 +56,7 @@ def tile_picked_pqjfrackindddot_none_p_kernel(
 
         def load_scales(name, src, width):
             tile = sb(name, width, U8)
-            rows = src[0].bitcast(I32).unsqueeze(1).to_broadcast([16, 8, width // 4])
+            rows = src[0].bitcast(I32).unsqueeze(1).to_broadcast([BLOCKS, BLOCK_ROWS, width // 4])
             nc.sync.dma_start(tile[:].bitcast(I32), rows)
             return tile
 
@@ -52,19 +65,41 @@ def tile_picked_pqjfrackindddot_none_p_kernel(
             nc.sync.dma_start(tile[:], src[0].rearrange("p n t -> p (n t)").bitcast(I32))
             return tile
 
-        def rows_of_tile(src, t):
-            return src.rearrange("(b t r) c -> t b r c", t=PACK, r=8)[t]
+        def plane_rows(src, t):
+            return src.rearrange("(b t r) c -> t b r c", t=PLANES, r=BLOCK_ROWS)[t]
 
-        def load_weight(tile, src, tiles):
-            for t in tiles:
-                nc.sync.dma_start(tile[:, t * N : (t + 1) * N], rows_of_tile(src, t))
+        def load_weight(tile, src, which):
+            for t in which:
+                nc.sync.dma_start(tile[:, t * N : (t + 1) * N], plane_rows(src, t))
 
-        def load_gain(name, src, offset):
-            spread = placed(name + "_spread", PACK * 8, F32, offset)
+        def load_gain(name, src):
+            tile = sb(name, PLANES * GAIN_STEP, F32)
             with nc.allow_non_contiguous_dma(reason="one gain for each partition"):
-                for t in range(PACK):
-                    nc.sync.dma_start(spread[:, 8 * t : 8 * t + 1], rows_of_tile(src, t))
-            return spread[:, 0 : PACK * 8 : 8]
+                for t in range(PLANES):
+                    nc.sync.dma_start(tile[:, GAIN_STEP * t : GAIN_STEP * t + 1], plane_rows(src, t))
+            return tile[:, 0 : PLANES * GAIN_STEP : GAIN_STEP]
+
+        def window(tile):
+            nc.gpsimd.memset(tile[:, S:], 0.0)
+            return tile
+
+        def interleaved(tile):
+            return tile[:].rearrange("p (c i t) -> p c t i", i=RUN, t=PLANES)
+
+        def planes(tile):
+            return tile[:].rearrange("p (t c i) -> p c t i", i=RUN, t=PLANES)
+
+        def col(t):
+            return slice(t * S, (t + 1) * S)
+
+        def half(u):
+            return slice(2 * u * S, 2 * (u + 1) * S)
+
+        def quantize(codes, scales, rounded):
+            nc.vector.quantize_mx(out=codes.bitcast(FP8X4), scales=scales, in_=rounded)
+
+        def absolute(dst, src):
+            nc.vector.scalar_tensor_tensor(dst, src, -1.0, src, ALU.mult, ALU.max)
 
         x_sc = load_scales("x_sc", x_scales, T)
         two_l = load_list("two_l", two)
@@ -72,11 +107,9 @@ def tile_picked_pqjfrackindddot_none_p_kernel(
         d_sc = load_scales("d_sc", d_scales, G)
         k2_l = load_list("k2_l", k2)
         k1_l = load_list("k1_l", k1)
-        row = 4 * J
-        x_w = placed("x_w", T, I32, 2 * row + 128)
-        nc.sync.dma_start(x_w[:], x_words[0].rearrange("p n t -> p (n t)").bitcast(I32))
+        x_w = load_words("x_w", x_words, T)
         d_w = load_words("d_w", d_words, G)
-        w2_raw = sb("w2_raw", PACK * N, F32)
+        w2_raw = sb("w2_raw", PLANES * N, F32)
         load_weight(w2_raw, w2, (0, 1))
         n4_l = load_list("n4_l", n4)
         n3_l = load_list("n3_l", n3)
@@ -87,77 +120,54 @@ def tile_picked_pqjfrackindddot_none_p_kernel(
         n5_l = load_list("n5_l", n5)
         n6_l = load_list("n6_l", n6)
 
-        def windows(name, base=None):
-            if base is None:
-                tiles = [sb(name + str(t), S + SPARE, F32) for t in range(PACK)]
-            else:
-                tiles = [placed(name + str(t), S + SPARE, F32, base + t * 1088) for t in range(PACK)]
-            for tile in tiles:
-                nc.gpsimd.memset(tile[:, S:], 0.0)
-            return tiles
-
         eight = sb("eight", 1, F32)
         nc.gpsimd.memset(eight[:], 8.0)
         warm = sb("warm", 1, F32)
         nc.scalar.activation(warm[:], eight[:], ACT.Abs_reciprocal_sqrt, bias=eight[:])
-        a_win = windows("a_win", 6 * row)
-        b_win = windows("b_win")
-        h_win = windows("h_win")
+        a_win = [
+            window(placed("a_win" + str(t), S + SPARE, F32, A_WINDOWS + t * WINDOW_PITCH)) for t in range(PLANES)
+        ]
+        b_win = [window(sb("b_win" + str(t), S + SPARE, F32)) for t in range(PLANES)]
+        h_win = [window(sb("h_win" + str(m), S + SPARE, F32)) for m in range(PLANES)]
 
-        sc_picked = placed("sc_picked", 2 * H + 2 * S, U8, row // 2)
+        sc_picked = sb("sc_picked", 2 * H + 2 * S, U8)
         nc.vector.tensor_copy(sc_picked[:, 2 * H + S :], x_sc[:].indirect(two_l[:]))
         nc.vector.tensor_copy(sc_picked[:, 2 * H : 2 * H + S], x_sc[:].indirect(offs_l[:]))
         nc.vector.tensor_copy(sc_picked[:, H : 2 * H], d_sc[:].indirect(k2_l[:]))
         nc.vector.tensor_copy(sc_picked[:, 0:H], d_sc[:].indirect(k1_l[:]))
-        sc = sb("sc", 2 * H + 2 * S, U8)
+        sc = sb("sc", 2 * H + 2 * S, U8, on="d_sc")
         nc.vector.tensor_copy(
-            sc[:, : 2 * H].bitcast(I32).rearrange("p (l t b w) -> p l t b w", l=2, t=PACK, w=2),
-            sc_picked[:, : 2 * H].bitcast(I32).rearrange("p (l b t w) -> p l t b w", l=2, t=PACK, w=2),
+            sc[:, : 2 * H].bitcast(I32).rearrange("p (l t b w) -> p l t b w", l=2, t=PLANES, w=2),
+            sc_picked[:, : 2 * H].bitcast(I32).rearrange("p (l b t w) -> p l t b w", l=2, t=PLANES, w=2),
         )
         nc.vector.tensor_copy(sc[:, 2 * H :].bitcast(I32), sc_picked[:, 2 * H :].bitcast(I32))
-        for i in range(1, 4):
-            nc.sync.dma_start(sc[i:P:32, :].bitcast(I32), sc[8 * i : P : 32, :].bitcast(I32))
+        for i in range(1, QUADRANT // BLOCK_ROWS):
+            nc.sync.dma_start(sc[i:P:QUADRANT, :].bitcast(I32), sc[BLOCK_ROWS * i : P : QUADRANT, :].bitcast(I32))
 
-        def load_tab(t):
-            tile = placed("tab_win" + str(t), J, F32, t * row + (128 if t else 0))
-            nc.sync.dma_start(tile[:], rows_of_tile(tab, t))
-            return tile
+        tab_win = [sb("tab_win" + str(t), J, F32) for t in range(PLANES)]
+        for t in range(PLANES):
+            nc.sync.dma_start(tab_win[t][:], plane_rows(tab, t))
 
-        tab_win = [load_tab(0), load_tab(1)]
-
-        def interleaved(tile):
-            return tile[:].rearrange("p (c i t) -> p c t i", i=4, t=PACK)
-
-        def planes(tile):
-            return tile[:].rearrange("p (t c i) -> p c t i", i=4, t=PACK)
-
-        def quantize(name, grouped, width, offset=None):
-            if offset is None:
-                codes = sb(name + "_codes", width, U32)
-            else:
-                codes = placed(name + "_codes", width, U32, offset)
-            scales = sb(name + "_scales", width, U8)
-            nc.vector.quantize_mx(out=codes[:].bitcast(FP8X4), scales=scales[:], in_=grouped[:])
-            return codes, scales
-
-        w2_bf = sb("w2_bf", PACK * N, BF16)
+        w2_bf = sb("w2_bf", PLANES * N, BF16)
         nc.scalar.copy(interleaved(w2_bf), planes(w2_raw))
 
-        def pick_tokens(name, x_list):
-            tokens = sb(name + "_tokens", S, U32)
-            nc.vector.tensor_copy(tokens[:], x_w[:].bitcast(U32).indirect(x_list[:]))
-            return tokens
-
-        def first_product(name, d_list, tokens, side, picked, outs):
-            nc.vector.tensor_copy(picked[:], d_w[:].bitcast(U32).indirect(d_list[:]))
+        def first_product(name, d_list, x_list, side, picked, tokens, sums):
             dealt = sb(name + "_dealt", H, I32)
-            nc.vector.tensor_copy(
-                dealt[:].rearrange("p (t b r) -> p t b r", t=PACK, r=8),
-                picked[:].bitcast(I32).rearrange("p (b t r) -> p t b r", t=PACK, r=8),
-            )
-            for t in range(PACK):
+            blocks = BLOCKS // len(picked)
+            columns = H // LIST_ROWS // len(picked)
+            for c, piece in enumerate(picked):
+                offsets = d_list[:, c * columns : (c + 1) * columns]
+                nc.vector.tensor_copy(piece[:], d_w[:].bitcast(U32).indirect(offsets))
+            nc.vector.tensor_copy(tokens[:], x_w[:].bitcast(U32).indirect(x_list[:]))
+            by_plane = dealt[:].rearrange("p (t b r) -> p t b r", t=PLANES, r=BLOCK_ROWS)
+            for c, piece in enumerate(picked):
+                nc.vector.tensor_copy(
+                    by_plane[:, :, c * blocks : (c + 1) * blocks, :],
+                    piece[:].bitcast(I32).rearrange("p (b t r) -> p t b r", t=PLANES, r=BLOCK_ROWS),
+                )
+            for t in range(PLANES):
                 nc.tensor.matmul_mx(
-                    out=outs[t],
+                    out=sums[t],
                     lhsT=dealt[:, t * P : (t + 1) * P].bitcast(FP8X4),
                     lhsT_scale=sc[:, side * H + t * P : side * H + (t + 1) * P],
                     rhs=tokens[:].bitcast(FP8X4),
@@ -166,87 +176,61 @@ def tile_picked_pqjfrackindddot_none_p_kernel(
                     stop=True,
                 )
 
-        b_tokens = pick_tokens("b", two_l)
-        a_tokens = pick_tokens("a", offs_l)
-        tab_win.extend([load_tab(2), load_tab(3)])
-        b_bank = [psum.tile([P, S], F32, name="b_bank" + str(t), tag="single" + str(t)) for t in range(PACK)]
+        b_bank = [psum.tile([P, S], F32, name="b_bank" + str(t), tag="single" + str(t)) for t in range(PLANES)]
         a_bank = [psum.tile([P, 2 * S], F32, name="a_bank" + str(u)) for u in range(2)]
-        a_sums = [a_bank[t // 2][:, (t % 2) * S : (t % 2 + 1) * S] for t in range(PACK)]
-        first_product("b", k2_l, b_tokens, 1, placed("b_picked", H, U32, 12 * row), [bank[:] for bank in b_bank])
-        gm_t = sb("gm_t", PACK, F32)
-        nc.gpsimd.tensor_copy(gm_t[:], load_gain("gm_t", gm, 12 * row))
-        gn_t = load_gain("gn_t", gn, 12 * row + 128)
-        first_product("a", k1_l, a_tokens, 0, placed("a_picked", H, U32, 12 * row + row // 2), a_sums)
-        w1_raw = sb("w1_raw", PACK * N, F32, "d_w")
-        load_weight(w1_raw, w1, range(PACK))
+        a_sums = [a_bank[t // 2][:, col(t % 2)] for t in range(PLANES)]
+        b_picked = [placed("b_picked", H, U32, PICKED_AREA)]
+        first_product("b", k2_l, two_l, 1, b_picked, sb("b_tokens", S, U32), [bank[:] for bank in b_bank])
+        gm_t = sb("gm_t", PLANES, F32)
+        nc.gpsimd.tensor_copy(gm_t[:], load_gain("gm_spread", gm))
+        gn_t = load_gain("gn_spread", gn)
+        a_picked = [sb("a_picked0", H // 2, U32), placed("a_picked1", H // 2, U32, PICKED_AREA + KIB)]
+        first_product("a", k1_l, offs_l, 0, a_picked, placed("a_tokens", S, U32, PICKED_AREA), a_sums)
+        w1_raw = sb("w1_raw", PLANES * N, F32)
+        load_weight(w1_raw, w1, range(PLANES))
 
-        def col(t):
-            return slice(t * S, (t + 1) * S)
-
-        def half(u):
-            return slice(2 * u * S, 2 * (u + 1) * S)
-
-        bt_n4 = sb("bt_n4", PACK * S, F32)
-        taken = sb("taken", PACK * S, F32)
-        left = sb("left", PACK * S, F32)
-        left_size = sb("left_size", PACK * S, F32)
-        at_n1 = sb("at_n1", PACK * S, F32)
-        at_n2 = sb("at_n2", PACK * S, F32)
-        numer = sb("numer", PACK * S, F32)
-        part = sb("part", PACK * S, F32)
-        for t in range(PACK):
+        b_at_n4 = sb("b_at_n4", PLANES * S, F32)
+        taken = sb("taken", PLANES * S, F32)
+        left = sb("left", PLANES * S, F32)
+        left_size = sb("left_size", PLANES * S, F32)
+        for t in range(PLANES):
             nc.scalar.activation(b_win[t][:, :S], b_bank[t][:], ACT.Copy, scale=0.0625)
+        for t in range(PLANES):
+            nc.scalar.activation(b_at_n4[:, col(t)], b_win[t][:].indirect(n4_l[:]), ACT.Copy)
+            nc.vector.tensor_tensor(taken[:, col(t)], tab_win[t][:].indirect(n3_l[:]), b_win[t][:, :S], ALU.subtract)
+        w2_codes = sb("w2_codes", N, U32)
+        w2_scales = sb("w2_scales", N, U8)
+        quantize(w2_codes[:], w2_scales[:], w2_bf[:])
         for u in range(2):
-            for t in (2 * u, 2 * u + 1):
-                nc.scalar.activation(bt_n4[:, col(t)], b_win[t][:].indirect(n4_l[:]), ACT.Copy)
-                nc.vector.tensor_tensor(taken[:, col(t)], tab_win[t][:].indirect(n3_l[:]), b_win[t][:, :S], ALU.subtract)
-        w2_codes, w2_scales = quantize("w2", w2_bf, N, 13 * row)
+            nc.vector.tensor_tensor(left[:, half(u)], taken[:, half(u)], b_at_n4[:, half(u)], ALU.add)
         for u in range(2):
-            nc.vector.tensor_tensor(left[:, half(u)], taken[:, half(u)], bt_n4[:, half(u)], ALU.add)
-        for u in range(2):
-            nc.vector.scalar_tensor_tensor(
-                left_size[:, half(u)], left[:, half(u)], -1.0, left[:, half(u)], ALU.mult, ALU.max
-            )
+            absolute(left_size[:, half(u)], left[:, half(u)])
 
-        size = [sb("size0", 2 * S, F32), placed("size1", 2 * S, F32, 9 * row + row // 2)]
-        for t in range(PACK):
+        a_at_n2 = sb("a_at_n2", PLANES * S, F32)
+        size = [sb("size0", 2 * S, F32), placed("size1", 2 * S, F32, SIZE_AREA)]
+        for t in range(PLANES):
             nc.scalar.copy(a_win[t][:, :S], a_sums[t])
-        for t in range(PACK):
-            nc.scalar.activation(at_n2[:, col(t)], a_win[t][:].indirect(n2_l[:]), ACT.Copy)
+        for t in range(PLANES):
+            nc.scalar.activation(a_at_n2[:, col(t)], a_win[t][:].indirect(n2_l[:]), ACT.Copy)
 
-        def distance(u, tag):
-            diff = sb("diff" + str(u), 2 * S, F32, tag)
-            nc.vector.tensor_tensor(diff[:], at_n2[:, half(u)], a_bank[u][:], ALU.subtract)
-            nc.vector.scalar_tensor_tensor(size[u][:], diff[:], -1.0, diff[:], ALU.mult, ALU.max)
+        def distance(u, diff):
+            nc.vector.tensor_tensor(diff[:], a_at_n2[:, half(u)], a_bank[u][:], ALU.subtract)
+            absolute(size[u][:], diff[:])
 
-        distance(0, "taken")
-        z2_bf = sb("z2_bf", PACK * S, BF16)
-        gm_wide = gm_t[:].unsqueeze(1).unsqueeze(3).to_broadcast([P, S // 4, PACK, 4])
+        distance(0, sb("diff0", 2 * S, F32, on="taken"))
+        z2_bf = sb("z2_bf", PLANES * S, BF16)
+        gm_wide = gm_t[:].unsqueeze(1).unsqueeze(3).to_broadcast([P, S // RUN, PLANES, RUN])
         nc.vector.tensor_tensor(interleaved(z2_bf), planes(left_size), gm_wide, ALU.mult)
-        z2_codes, z2_scales = quantize("z2", z2_bf, S)
-        distance(1, "left_size")
+        distance(1, sb("diff1", 2 * S, F32, on="left_size"))
 
-        h_bank = [psum.tile([P, S], F32, name="h_bank" + str(m), tag="single" + str(m)) for m in range(PACK)]
-
-        def last_product(codes, scales, moving, moving_scales, first):
-            for m in range(PACK):
-                nc.tensor.matmul_mx(
-                    out=h_bank[m][:],
-                    lhsT=codes[:, m * P : (m + 1) * P].bitcast(FP8X4),
-                    lhsT_scale=scales[:, m * P : (m + 1) * P],
-                    rhs=moving[:].bitcast(FP8X4),
-                    rhs_scale=moving_scales[:],
-                    start=first,
-                    stop=not first,
-                )
-
-        last_product(w2_codes, w2_scales, z2_codes, z2_scales, True)
-
-        root = placed("root", PACK * S, F32, 6 * row + 2 * 1088 - 2 * row)
+        a_at_n1 = sb("a_at_n1", PLANES * S, F32)
+        numer = sb("numer", PLANES * S, F32)
+        part = sb("part", PLANES * S, F32)
+        root = placed("root", PLANES * S, F32, A_WINDOWS + 2 * WINDOW_PITCH - 4 * KIB)
         for u in range(2):
             for t in (2 * u, 2 * u + 1):
-                nc.scalar.activation(at_n1[:, col(t)], a_win[t][:].indirect(n1_l[:]), ACT.Copy)
-            nc.vector.tensor_tensor(numer[:, half(u)], a_bank[u][:], at_n1[:, half(u)], ALU.subtract)
+                nc.scalar.activation(a_at_n1[:, col(t)], a_win[t][:].indirect(n1_l[:]), ACT.Copy)
+            nc.vector.tensor_tensor(numer[:, half(u)], a_bank[u][:], a_at_n1[:, half(u)], ALU.subtract)
         for u in range(2):
             nc.scalar.activation(root[:, half(u)], size[u][:], ACT.Abs_reciprocal_sqrt, bias=eight[:])
             for t in (2 * u, 2 * u + 1):
@@ -254,38 +238,68 @@ def tile_picked_pqjfrackindddot_none_p_kernel(
                     part[:, col(t)], numer[:, col(t)], gn_t[:, t : t + 1], root[:, col(t)], ALU.mult, ALU.mult
                 )
 
-        w1_codes = sb("w1_codes", N, U32, "numer")
-        w1_scales = sb("w1_scales", N, U8)
-        w1_bf = [placed("w1_bf" + str(u), 2 * N, BF16, (9 + u) * row) for u in range(2)]
-        wide = N // 8
+        h_bank = [psum.tile([P, S], F32, name="h_bank" + str(m), tag="single" + str(m)) for m in range(PLANES)]
+
+        def last_product(w_codes, w_scales, codes, scales, first):
+            for m in range(PLANES):
+                nc.tensor.matmul_mx(
+                    out=h_bank[m][:],
+                    lhsT=w_codes[:, m * P : (m + 1) * P].bitcast(FP8X4),
+                    lhsT_scale=w_scales[:, m * P : (m + 1) * P],
+                    rhs=codes[:].bitcast(FP8X4),
+                    rhs_scale=scales[:],
+                    start=first,
+                    stop=not first,
+                )
+
+        z2_codes = placed("z2_codes", S, U32, SIZE_AREA + ALIGN)
+        z2_scales = sb("z2_scales", S, U8)
+        quantize(z2_codes[:], z2_scales[:], z2_bf[:])
+        last_product(w2_codes, w2_scales, z2_codes, z2_scales, True)
+
+        w1_bf = [
+            placed("w1_bf0", 2 * N, BF16, SIZE_AREA - 2 * KIB + ALIGN),
+            placed("w1_bf1", 2 * N, BF16, SIZE_AREA + 2 * KIB - ALIGN),
+        ]
+        runs = N // RUN // 2
         for u in range(2):
-            nc.scalar.copy(interleaved(w1_bf[u]), planes(w1_raw)[:, u * wide : (u + 1) * wide])
+            nc.scalar.copy(interleaved(w1_bf[u]), planes(w1_raw)[:, u * runs : (u + 1) * runs])
+        w1_codes = sb("w1_codes", N, U32, on="numer")
+        w1_scales = sb("w1_scales", N, U8)
 
         def quantize_w1(u):
-            nc.vector.quantize_mx(
-                out=w1_codes[:, u * N // 2 : (u + 1) * N // 2].bitcast(FP8X4),
-                scales=w1_scales[:, u * N // 2 : (u + 1) * N // 2],
-                in_=w1_bf[u][:],
-            )
+            columns = slice(u * N // 2, (u + 1) * N // 2)
+            quantize(w1_codes[:, columns], w1_scales[:, columns], w1_bf[u][:])
 
-        z_bf = sb("z_bf", PACK * S, BF16)
+        z_bf = sb("z_bf", PLANES * S, BF16)
+        z_codes = sb("z_codes", S, U32)
+        z_scales = sb("z_scales", S, U8)
         nc.vector.tensor_tensor(interleaved(z_bf), planes(part), planes(root), ALU.mult)
         quantize_w1(0)
-        z_codes, z_scales = quantize("z", z_bf, S)
+        quantize(z_codes[:], z_scales[:], z_bf[:])
         quantize_w1(1)
         last_product(w1_codes, w1_scales, z_codes, z_scales, False)
 
-        for m in range(PACK):
+        for m in range(PLANES):
             nc.vector.tensor_copy(h_win[m][:, :S], h_bank[m][:])
-        for m in range(PACK):
-            at_n7 = sb("at_n7_" + str(m), S, F32)
-            at_n5 = sb("at_n5_" + str(m), S, F32)
-            far = sb("far" + str(m), S, F32)
-            near = sb("near" + str(m), S, F32)
+        far = [sb("far" + str(m), S, F32) for m in range(PLANES)]
+        near = [sb("near" + str(m), S, F32) for m in range(PLANES)]
+
+        def products(m):
+            h_at_n7 = sb("h_at_n7_" + str(m), S, F32)
+            h_at_n5 = sb("h_at_n5_" + str(m), S, F32)
+            nc.scalar.activation(h_at_n7[:], h_win[m][:].indirect(n7_l[:]), ACT.Copy)
+            nc.scalar.activation(h_at_n5[:], h_win[m][:].indirect(n5_l[:]), ACT.Copy)
+            nc.vector.tensor_tensor(far[m][:], h_win[m][:].indirect(n6_l[:]), h_at_n7[:], ALU.mult)
+            nc.vector.scalar_tensor_tensor(near[m][:], h_at_n5[:], 0.75, h_bank[m][:], ALU.mult, ALU.mult)
+
+        def finish(m):
             result = sb("result" + str(m), S, F32)
-            nc.scalar.activation(at_n7[:], h_win[m][:].indirect(n7_l[:]), ACT.Copy)
-            nc.scalar.activation(at_n5[:], h_win[m][:].indirect(n5_l[:]), ACT.Copy)
-            nc.vector.tensor_tensor(far[:], h_win[m][:].indirect(n6_l[:]), at_n7[:], ALU.mult)
-            nc.vector.scalar_tensor_tensor(near[:], at_n5[:], 0.75, h_bank[m][:], ALU.mult, ALU.mult)
-            nc.vector.scalar_tensor_tensor(result[:], far[:], 0.75, near[:], ALU.mult, ALU.add)
+            nc.vector.scalar_tensor_tensor(result[:], far[m][:], 0.75, near[m][:], ALU.mult, ALU.add)
             nc.sync.dma_start(out[m * P : (m + 1) * P, :], result[:])
+
+        products(0)
+        for m in range(1, PLANES):
+            products(m)
+            finish(m - 1)
+        finish(PLANES - 1)

from contextlib import ExitStack

import concourse.mybir as mybir

T, S, N, G, H, J = 1024, 256, 512, 2048, 512, 512
FLOPS = 4 * 2 * 512 * 512 * 256

F32 = mybir.dt.float32
BF16 = mybir.dt.bfloat16
U32 = mybir.dt.uint32
I32 = mybir.dt.int32
U16 = mybir.dt.uint16
U8 = mybir.dt.uint8
FP8X4 = mybir.dt.float8_e4m3fn_x4
ALU = mybir.AluOpType
ACT = mybir.ActivationFunctionType

P = 128
PLANES = 4
BLOCK_ROWS = 8
BLOCKS = P // BLOCK_ROWS
QUADRANT = 32
LIST_ROWS = 16
RUN = 4
SPARE = 8
GAIN_STEP = 8
ALIGN = 64

KIB = 1024
WINDOW_PITCH = 1088
A_WINDOWS = 4 * KIB
SIZE_AREA = 12 * KIB
PICKED_AREA = 18 * KIB


def tile_picked_pqjfrackindddot_none_p_kernel(
    tc, x_words, x_scales, d_words, d_scales, tab, gn, gm, w1, w2,
    offs, k1, two, k2, n1, n2, n3, n4, n5, n6, n7, out,
):
    nc = tc.nc
    with ExitStack() as ctx:
        keep = ctx.enter_context(tc.tile_pool(name="keep", bufs=1))
        by_hand = ctx.enter_context(tc.tile_pool(name="by_hand", bufs=1))
        psum = ctx.enter_context(tc.psum_pool(name="psum", bufs=1))

        def sb(name, width, dtype, on=None):
            return keep.tile([P, width], dtype, name=name, tag=on or name, align_bytes=ALIGN)

        def placed(name, width, dtype, offset):
            return by_hand.tile([P, width], dtype, name=name, offset=offset, align_bytes=ALIGN)

        def load_list(name, src):
            tile = keep.tile([P, src.shape[1]], U16, name=name)
            nc.sync.dma_start(tile[:], src)
            return tile

        def load_scales(name, src, width):
            tile = sb(name, width, U8)
            rows = src[0].bitcast(I32).unsqueeze(1).to_broadcast([BLOCKS, BLOCK_ROWS, width // 4])
            nc.sync.dma_start(tile[:].bitcast(I32), rows)
            return tile

        def load_words(name, src, width):
            tile = sb(name, width, I32)
            nc.sync.dma_start(tile[:], src[0].rearrange("p n t -> p (n t)").bitcast(I32))
            return tile

        def plane_rows(src, t):
            return src.rearrange("(b t r) c -> t b r c", t=PLANES, r=BLOCK_ROWS)[t]

        def load_weight(tile, src, which):
            for t in which:
                nc.sync.dma_start(tile[:, t * N : (t + 1) * N], plane_rows(src, t))

        def load_gain(name, src):
            tile = sb(name, PLANES * GAIN_STEP, F32)
            with nc.allow_non_contiguous_dma(reason="one gain for each partition"):
                for t in range(PLANES):
                    nc.sync.dma_start(tile[:, GAIN_STEP * t : GAIN_STEP * t + 1], plane_rows(src, t))
            return tile[:, 0 : PLANES * GAIN_STEP : GAIN_STEP]

        def window(tile):
            nc.gpsimd.memset(tile[:, S:], 0.0)
            return tile

        def interleaved(tile):
            return tile[:].rearrange("p (c i t) -> p c t i", i=RUN, t=PLANES)

        def planes(tile):
            return tile[:].rearrange("p (t c i) -> p c t i", i=RUN, t=PLANES)

        def col(t):
            return slice(t * S, (t + 1) * S)

        def half(u):
            return slice(2 * u * S, 2 * (u + 1) * S)

        def quantize(codes, scales, rounded):
            nc.vector.quantize_mx(out=codes.bitcast(FP8X4), scales=scales, in_=rounded)

        def absolute(dst, src):
            nc.vector.scalar_tensor_tensor(dst, src, -1.0, src, ALU.mult, ALU.max)

        x_sc = load_scales("x_sc", x_scales, T)
        two_l = load_list("two_l", two)
        offs_l = load_list("offs_l", offs)
        d_sc = load_scales("d_sc", d_scales, G)
        k2_l = load_list("k2_l", k2)
        k1_l = load_list("k1_l", k1)
        x_w = load_words("x_w", x_words, T)
        d_w = load_words("d_w", d_words, G)
        w2_raw = sb("w2_raw", PLANES * N, F32)
        load_weight(w2_raw, w2, (0, 1))
        n4_l = load_list("n4_l", n4)
        n3_l = load_list("n3_l", n3)
        n2_l = load_list("n2_l", n2)
        n1_l = load_list("n1_l", n1)
        load_weight(w2_raw, w2, (2, 3))
        n7_l = load_list("n7_l", n7)
        n5_l = load_list("n5_l", n5)
        n6_l = load_list("n6_l", n6)

        eight = sb("eight", 1, F32)
        nc.gpsimd.memset(eight[:], 8.0)
        warm = sb("warm", 1, F32)
        nc.scalar.activation(warm[:], eight[:], ACT.Abs_reciprocal_sqrt, bias=eight[:])
        a_win = [
            window(placed("a_win" + str(t), S + SPARE, F32, A_WINDOWS + t * WINDOW_PITCH)) for t in range(PLANES)
        ]
        b_win = [window(sb("b_win" + str(t), S + SPARE, F32)) for t in range(PLANES)]
        h_win = [window(sb("h_win" + str(m), S + SPARE, F32)) for m in range(PLANES)]

        sc_picked = sb("sc_picked", 2 * H + 2 * S, U8)
        nc.vector.tensor_copy(sc_picked[:, 2 * H + S :], x_sc[:].indirect(two_l[:]))
        nc.vector.tensor_copy(sc_picked[:, 2 * H : 2 * H + S], x_sc[:].indirect(offs_l[:]))
        nc.vector.tensor_copy(sc_picked[:, H : 2 * H], d_sc[:].indirect(k2_l[:]))
        nc.vector.tensor_copy(sc_picked[:, 0:H], d_sc[:].indirect(k1_l[:]))
        sc = sb("sc", 2 * H + 2 * S, U8, on="d_sc")
        nc.vector.tensor_copy(
            sc[:, : 2 * H].bitcast(I32).rearrange("p (l t b w) -> p l t b w", l=2, t=PLANES, w=2),
            sc_picked[:, : 2 * H].bitcast(I32).rearrange("p (l b t w) -> p l t b w", l=2, t=PLANES, w=2),
        )
        nc.vector.tensor_copy(sc[:, 2 * H :].bitcast(I32), sc_picked[:, 2 * H :].bitcast(I32))
        for i in range(1, QUADRANT // BLOCK_ROWS):
            nc.sync.dma_start(sc[i:P:QUADRANT, :].bitcast(I32), sc[BLOCK_ROWS * i : P : QUADRANT, :].bitcast(I32))

        tab_win = [sb("tab_win" + str(t), J, F32) for t in range(PLANES)]
        for t in range(PLANES):
            nc.sync.dma_start(tab_win[t][:], plane_rows(tab, t))

        w2_bf = sb("w2_bf", PLANES * N, BF16)
        nc.scalar.copy(interleaved(w2_bf), planes(w2_raw))

        def first_product(name, d_list, x_list, side, picked, tokens, sums):
            dealt = sb(name + "_dealt", H, I32)
            blocks = BLOCKS // len(picked)
            columns = H // LIST_ROWS // len(picked)
            for c, piece in enumerate(picked):
                offsets = d_list[:, c * columns : (c + 1) * columns]
                nc.vector.tensor_copy(piece[:], d_w[:].bitcast(U32).indirect(offsets))
            nc.vector.tensor_copy(tokens[:], x_w[:].bitcast(U32).indirect(x_list[:]))
            by_plane = dealt[:].rearrange("p (t b r) -> p t b r", t=PLANES, r=BLOCK_ROWS)
            for c, piece in enumerate(picked):
                nc.vector.tensor_copy(
                    by_plane[:, :, c * blocks : (c + 1) * blocks, :],
                    piece[:].bitcast(I32).rearrange("p (b t r) -> p t b r", t=PLANES, r=BLOCK_ROWS),
                )
            for t in range(PLANES):
                nc.tensor.matmul_mx(
                    out=sums[t],
                    lhsT=dealt[:, t * P : (t + 1) * P].bitcast(FP8X4),
                    lhsT_scale=sc[:, side * H + t * P : side * H + (t + 1) * P],
                    rhs=tokens[:].bitcast(FP8X4),
                    rhs_scale=sc[:, 2 * H + side * S : 2 * H + (side + 1) * S],
                    start=True,
                    stop=True,
                )

        b_bank = [psum.tile([P, S], F32, name="b_bank" + str(t), tag="single" + str(t)) for t in range(PLANES)]
        a_bank = [psum.tile([P, 2 * S], F32, name="a_bank" + str(u)) for u in range(2)]
        a_sums = [a_bank[t // 2][:, col(t % 2)] for t in range(PLANES)]
        b_picked = [placed("b_picked", H, U32, PICKED_AREA)]
        first_product("b", k2_l, two_l, 1, b_picked, sb("b_tokens", S, U32), [bank[:] for bank in b_bank])
        gm_t = sb("gm_t", PLANES, F32)
        nc.gpsimd.tensor_copy(gm_t[:], load_gain("gm_spread", gm))
        gn_t = load_gain("gn_spread", gn)
        a_picked = [sb("a_picked0", H // 2, U32), placed("a_picked1", H // 2, U32, PICKED_AREA + KIB)]
        first_product("a", k1_l, offs_l, 0, a_picked, placed("a_tokens", S, U32, PICKED_AREA), a_sums)
        w1_raw = sb("w1_raw", PLANES * N, F32)
        load_weight(w1_raw, w1, range(PLANES))

        b_at_n4 = sb("b_at_n4", PLANES * S, F32)
        taken = sb("taken", PLANES * S, F32)
        left = sb("left", PLANES * S, F32)
        left_size = sb("left_size", PLANES * S, F32)
        for t in range(PLANES):
            nc.scalar.activation(b_win[t][:, :S], b_bank[t][:], ACT.Copy, scale=0.0625)
        for t in range(PLANES):
            nc.scalar.activation(b_at_n4[:, col(t)], b_win[t][:].indirect(n4_l[:]), ACT.Copy)
            nc.vector.tensor_tensor(taken[:, col(t)], tab_win[t][:].indirect(n3_l[:]), b_win[t][:, :S], ALU.subtract)
        w2_codes = sb("w2_codes", N, U32)
        w2_scales = sb("w2_scales", N, U8)
        quantize(w2_codes[:], w2_scales[:], w2_bf[:])
        for u in range(2):
            nc.vector.tensor_tensor(left[:, half(u)], taken[:, half(u)], b_at_n4[:, half(u)], ALU.add)
        for u in range(2):
            absolute(left_size[:, half(u)], left[:, half(u)])

        a_at_n2 = sb("a_at_n2", PLANES * S, F32)
        size = [sb("size0", 2 * S, F32), placed("size1", 2 * S, F32, SIZE_AREA)]
        for t in range(PLANES):
            nc.scalar.copy(a_win[t][:, :S], a_sums[t])
        for t in range(PLANES):
            nc.scalar.activation(a_at_n2[:, col(t)], a_win[t][:].indirect(n2_l[:]), ACT.Copy)

        def distance(u, diff):
            nc.vector.tensor_tensor(diff[:], a_at_n2[:, half(u)], a_bank[u][:], ALU.subtract)
            absolute(size[u][:], diff[:])

        distance(0, sb("diff0", 2 * S, F32, on="taken"))
        z2_bf = sb("z2_bf", PLANES * S, BF16)
        gm_wide = gm_t[:].unsqueeze(1).unsqueeze(3).to_broadcast([P, S // RUN, PLANES, RUN])
        nc.vector.tensor_tensor(interleaved(z2_bf), planes(left_size), gm_wide, ALU.mult)
        distance(1, sb("diff1", 2 * S, F32, on="left_size"))

        a_at_n1 = sb("a_at_n1", PLANES * S, F32)
        numer = sb("numer", PLANES * S, F32)
        part = sb("part", PLANES * S, F32)
        root = placed("root", PLANES * S, F32, A_WINDOWS + 2 * WINDOW_PITCH - 4 * KIB)
        for u in range(2):
            for t in (2 * u, 2 * u + 1):
                nc.scalar.activation(a_at_n1[:, col(t)], a_win[t][:].indirect(n1_l[:]), ACT.Copy)
            nc.vector.tensor_tensor(numer[:, half(u)], a_bank[u][:], a_at_n1[:, half(u)], ALU.subtract)
        for u in range(2):
            nc.scalar.activation(root[:, half(u)], size[u][:], ACT.Abs_reciprocal_sqrt, bias=eight[:])
            for t in (2 * u, 2 * u + 1):
                nc.vector.scalar_tensor_tensor(
                    part[:, col(t)], numer[:, col(t)], gn_t[:, t : t + 1], root[:, col(t)], ALU.mult, ALU.mult
                )

        h_bank = [psum.tile([P, S], F32, name="h_bank" + str(m), tag="single" + str(m)) for m in range(PLANES)]

        def last_product(w_codes, w_scales, codes, scales, first):
            for m in range(PLANES):
                nc.tensor.matmul_mx(
                    out=h_bank[m][:],
                    lhsT=w_codes[:, m * P : (m + 1) * P].bitcast(FP8X4),
                    lhsT_scale=w_scales[:, m * P : (m + 1) * P],
                    rhs=codes[:].bitcast(FP8X4),
                    rhs_scale=scales[:],
                    start=first,
                    stop=not first,
                )

        z2_codes = placed("z2_codes", S, U32, SIZE_AREA + ALIGN)
        z2_scales = sb("z2_scales", S, U8)
        quantize(z2_codes[:], z2_scales[:], z2_bf[:])
        last_product(w2_codes, w2_scales, z2_codes, z2_scales, True)

        w1_bf = [
            placed("w1_bf0", 2 * N, BF16, SIZE_AREA - 2 * KIB + ALIGN),
            placed("w1_bf1", 2 * N, BF16, SIZE_AREA + 2 * KIB - ALIGN),
        ]
        runs = N // RUN // 2
        for u in range(2):
            nc.scalar.copy(interleaved(w1_bf[u]), planes(w1_raw)[:, u * runs : (u + 1) * runs])
        w1_codes = sb("w1_codes", N, U32, on="numer")
        w1_scales = sb("w1_scales", N, U8)

        def quantize_w1(u):
            columns = slice(u * N // 2, (u + 1) * N // 2)
            quantize(w1_codes[:, columns], w1_scales[:, columns], w1_bf[u][:])

        z_bf = sb("z_bf", PLANES * S, BF16)
        z_codes = sb("z_codes", S, U32)
        z_scales = sb("z_scales", S, U8)
        nc.vector.tensor_tensor(interleaved(z_bf), planes(part), planes(root), ALU.mult)
        quantize_w1(0)
        quantize(z_codes[:], z_scales[:], z_bf[:])
        quantize_w1(1)
        last_product(w1_codes, w1_scales, z_codes, z_scales, False)

        for m in range(PLANES):
            nc.vector.tensor_copy(h_win[m][:, :S], h_bank[m][:])
        far = [sb("far" + str(m), S, F32) for m in range(PLANES)]
        near = [sb("near" + str(m), S, F32) for m in range(PLANES)]

        def products(m):
            h_at_n7 = sb("h_at_n7_" + str(m), S, F32)
            h_at_n5 = sb("h_at_n5_" + str(m), S, F32)
            nc.scalar.activation(h_at_n7[:], h_win[m][:].indirect(n7_l[:]), ACT.Copy)
            nc.scalar.activation(h_at_n5[:], h_win[m][:].indirect(n5_l[:]), ACT.Copy)
            nc.vector.tensor_tensor(far[m][:], h_win[m][:].indirect(n6_l[:]), h_at_n7[:], ALU.mult)
            nc.vector.scalar_tensor_tensor(near[m][:], h_at_n5[:], 0.75, h_bank[m][:], ALU.mult, ALU.mult)

        def finish(m):
            result = sb("result" + str(m), S, F32)
            nc.vector.scalar_tensor_tensor(result[:], far[m][:], 0.75, near[m][:], ALU.mult, ALU.add)
            nc.sync.dma_start(out[m * P : (m + 1) * P, :], result[:])

        products(0)
        for m in range(1, PLANES):
            products(m)
            finish(m - 1)
        finish(PLANES - 1)
